import numpy as np, ml_dtypes
CORES = [66,74,82,90,194,202,210,218]
N = 8
import mx_ref
NC = 128
C2 = np.float32(0.328)
BF = ml_dtypes.bfloat16
def cut(t, i, w=512):
    return t[:, w * i:w * i + w]
def tile(rs):
    return np.stack(rs, axis=2).reshape(128, -1).astype(BF)
def pick(b):
    s = np.zeros((128, 128, 4), np.float32)
    s[np.arange(128), np.arange(128), b] = 1.0
    return mx_ref.quantize(s.reshape(128, 512).astype(BF))
def setup_inputs(rng):
    def f(*shape):
        return mx_ref.flush((rng.standard_normal(shape, dtype=np.float32) * np.exp2(rng.integers(-2, 3, shape[:-1] + (1,)))).astype(BF))
    return {"b": f(N, 128, N * 512), "x": f(N, 128, 4 * NC)}
def setup_inputs_blocks(rng):
    d = setup_inputs(rng)
    for k in ("b", "x"): d[k] = mx_ref.spread(d[k], rng, 2)
    return d
def setup_inputs_wide(rng):
    d = setup_inputs(rng)
    for k in ("b", "x"): d[k] = mx_ref.flush((d[k].astype(np.float32) * np.exp2(rng.integers(-4, 5, (N, 1, 1))).astype(np.float32)).astype(BF))
    return d
def reference(b, x, own=None):
    S = [pick(t) for t in range(4)]
    h = np.zeros((N, 128, 512), BF)
    for c in range(N):
        for r in range(N):
            q = mx_ref.quantize(cut(b[r], c))
            P = [mx_ref.matmul(S[t], q) for t in range(4)]
            Z = P if r == 0 else [z + p for z, p in zip(Z, P)]
        h[c] = tile([np.maximum(Z[t], 0) * C2 for t in range(4)])
    use = h if own is None else own["h"]
    H = [mx_ref.quantize(use[j]) for j in range(N)]
    y = np.zeros((N, 128, N * NC), np.float32)
    for r in range(N):
        qx = mx_ref.quantize(x[r])
        for j in range(N):
            y[r][:, NC * j:NC * j + NC] = mx_ref.matmul(H[j], qx)
    return {"h": h, "y": y}

@@ -1,0 +1,166 @@
+from concourse.bass import DstId, RemoteDMATransfer
+from concourse.mybir import dt, AluOpType, ActivationFunctionType
+
+N = 8
+W = 512
+C = 128
+C2 = 0.328
+
+SCRATCH = {
+    "bt": ("sbuf", [128, N * W], "bfloat16"),
+    "xt": ("sbuf", [128, W], "bfloat16"),
+    "eye": ("sbuf", [128, W + 4], "bfloat16"),
+    "ht": ("sbuf", [128, W], "bfloat16"),
+    "yt": ("sbuf", [128, N * C], "float32"),
+    "xq": ("sbuf", [128, C], "float8_e4m3fn_x4"), "xs": ("sbuf", [128, C], "uint8"),
+    "sq": ("sbuf", [128, 4 * C], "float8_e4m3fn_x4"), "ss": ("sbuf", [128, 4 * C], "uint8"),
+    "gq": ("sbuf", [128, N * C], "float8_e4m3fn_x4"), "gs": ("sbuf", [128, N * C], "uint8"),
+    "lq": ("sbuf", [128, N * C], "float8_e4m3fn_x4"), "ls": ("sbuf", [128, N * C], "uint8"),
+    "hq": ("sbuf", [128, N * C], "float8_e4m3fn_x4"), "hs": ("sbuf", [128, N * C], "uint8"),
+    "ps": ("psum", [128, 8 * 512], "float32"),
+}
+SEMAPHORES = (["ld%d" % i for i in range(5)] + ["ldx", "ones", "eye", "sdone", "qx", "relu", "qh", "sent1", "sent2", "hst", "yst", "yst2"]
+              + ["qp%d" % i for i in range(4)] + ["z%d" % i for i in range(4)] + ["arr%d" % i for i in range(N)]
+              + ["har%d" % i for i in range(N)] + ["ym%d" % i for i in range(N)] + ["yc%d" % i for i in range(N)])
+
+PAIRS = [(2, 3), (4, 5), (6, 7), (1, 0)]
+
+
+def rank_program(g, core, T, topo):
+    r = T.rank_of(core)
+    if r is None:
+        return
+    sem = T.sem
+
+    def cols(t, i, w=C, n=1):
+        return t[:, w * i:w * (i + n)]
+
+    def engines(dsts, parts):
+        m = 0xFFFFFFFF
+        for d in dsts:
+            m &= topo.mask(core, T.cores[d])
+        bits = [i for i in range(m.bit_length()) if (m >> i) & 1]
+        n = len(bits) // parts
+        return [sum(1 << i for i in bits[p * n:(p + 1) * n]) for p in range(parts)], n
+
+    def dst_id(d):
+        rid, pid = topo.addr(T.cores[d], core)
+        return DstId(rid=rid, pnc=pid)
+
+    first = [min(r ^ a, r ^ b) for a, b in PAIRS]
+
+    a = first[0]
+    g.sync.dma_start(cols(T.bt, a, W), cols(T.b, a, W)).then_inc(sem.ld0, 16)
+    g.scalar.dma_start(cols(T.bt, a + 1, W), cols(T.b, a + 1, W)).then_inc(sem.ld1, 16)
+    g.sync.dma_start(cols(T.bt, first[1], W, 2), cols(T.b, first[1], W, 2)).then_inc(sem.ld2, 16)
+    g.scalar.dma_start(cols(T.bt, first[2], W, 2), cols(T.b, first[2], W, 2)).then_inc(sem.ld3, 16)
+    g.sync.dma_start(cols(T.bt, first[3], W, 2), cols(T.b, first[3], W, 2)).then_inc(sem.ld4, 16)
+    g.scalar.dma_start(T.xt[:], T.x[:]).then_inc(sem.ldx, 16)
+
+    g.vector.memset(T.eye[:], 1.0).then_inc(sem.ones, 1)
+    g.wait_ge(sem.ones, 1)
+    g.affine_select(T.eye[:], T.eye[:], [[-1, W + 4]], AluOpType.is_equal, 0.0, 3, 4).then_inc(sem.eye, 1)
+
+    for i in range(4):
+        if i == 0:
+            g.vector.wait_ge(sem.ld0, 16)
+            g.vector.wait_ge(sem.ld1, 16)
+        else:
+            g.vector.wait_ge(sem["ld%d" % (i + 1)], 16)
+        f = first[i]
+        g.vector.quantize_mx(cols(T.gq, f, C, 2), cols(T.gs, f, C, 2), cols(T.bt, f, W, 2)).then_inc(sem["qp%d" % i], 1)
+        if i == 1:
+            g.vector.wait_ge(sem.eye, 1)
+            for b in range(4):
+                g.vector.quantize_mx(cols(T.sq, b), cols(T.ss, b), T.eye[:, 3 - b:3 - b + W]).then_inc(sem.sdone, 1)
+    g.vector.wait_ge(sem.ldx, 16)
+    g.vector.quantize_mx(T.xq[:], T.xs[:], T.xt[:]).then_inc(sem.qx, 1)
+
+    count = {}
+    sent1 = 0
+    for i in range(4):
+        dsts = [r ^ k for k in PAIRS[i] if k]
+        masks, n = engines(dsts, len(dsts))
+        g.wait_ge(sem["qp%d" % i], 1)
+        for codes in (True, False):
+            ts = []
+            for d, m in zip(dsts, masks):
+                src = cols(T.gq, d).bitcast(dt.uint8) if codes else cols(T.gs, d)
+                dst = cols(T.lq, r).bitcast(dt.uint8) if codes else cols(T.ls, r)
+                ts.append(RemoteDMATransfer(dst_ids=[dst_id(d)], srcs=[src], dsts=[dst], dma_engine_mask=m,
+                                            remote_sem=sem["arr%d" % r], alu_op=0))
+            g.remote_dma_fused(ts, local_sem=sem.sent1)
+            sent1 += n * len(dsts)
+        for k in PAIRS[i]:
+            count[k] = 2 * n
+
+    g.tensor.wait_ge(sem.sdone, 4)
+    order = [2, 3, 0, 4, 5, 6, 7, 1]
+    for i, k in enumerate(order):
+        s = r ^ k
+        if k:
+            g.tensor.wait_ge(sem["arr%d" % s], count[k])
+            q, p = cols(T.lq, s), cols(T.ls, s)
+        else:
+            g.tensor.wait_ge(sem.qp3, 1)
+            q, p = cols(T.gq, s), cols(T.gs, s)
+        for b in range(4):
+            mm = g.tensor.matmul_mx(T.ps[:, 512 * b:512 * b + C], cols(T.sq, b), cols(T.ss, b), q, p, i == 0, i == N - 1)
+            if i == N - 1:
+                mm.then_inc(sem["z%d" % b], 1)
+
+    for b in range(4):
+        z = T.ps[:, 512 * b:512 * b + C]
+        o = T.ht[:, b:W:4]
+        if b % 2 == 0:
+            g.vector.wait_ge(sem["z%d" % b], 1)
+            g.vector.tensor_scalar(o, z, 0.0, C2, AluOpType.max, AluOpType.mult).then_inc(sem.relu, 1)
+        else:
+            g.scalar.wait_ge(sem["z%d" % b], 1)
+            g.scalar.activation(o, z, ActivationFunctionType.Relu, scale=C2).then_inc(sem.relu, 1)
+    g.vector.wait_ge(sem.relu, 4)
+    g.vector.quantize_mx(cols(T.hq, r), cols(T.hs, r), T.ht[:]).then_inc(sem.qh, 1)
+    g.sync.wait_ge(sem.relu, 4)
+    g.sync.dma_start(T.h[:], T.ht[:]).then_inc(sem.hst, 16)
+
+    g.wait_ge(sem.qh, 1)
+    sent2 = 0
+    for ks in ((2, 3, 4, 5), (6, 7, 1)):
+        dsts = [r ^ k for k in ks]
+        masks, n = engines(dsts, 1)
+        for codes in (True, False):
+            side = cols(T.hq, r).bitcast(dt.uint8) if codes else cols(T.hs, r)
+            g.remote_dma_fused([RemoteDMATransfer(dst_ids=[dst_id(d) for d in dsts], srcs=[side], dsts=[side for d in dsts],
+                                                  dma_engine_mask=masks[0], remote_sem=sem["har%d" % r], alu_op=0)], local_sem=sem.sent2)
+            sent2 += n
+        got = 2 * n
+
+    order = [0, 2, 3, 4, 5, 6, 7, 1]
+    g.tensor.wait_ge(sem.qx, 1)
+    for i, k in enumerate(order):
+        j = r ^ k
+        bank = (i + 4) % 8
+        out = T.ps[:, 512 * bank:512 * bank + C]
+        if k:
+            g.tensor.wait_ge(sem["har%d" % j], got)
+        else:
+            g.tensor.wait_ge(sem.qh, 1)
+        g.tensor.matmul_mx(out, cols(T.hq, j), cols(T.hs, j), T.xq[:], T.xs[:], True, True).then_inc(sem["ym%d" % j], 1)
+        if i % 2 == 0:
+            g.vector.wait_ge(sem["ym%d" % j], 1)
+            g.vector.tensor_copy(cols(T.yt, j), out).then_inc(sem["yc%d" % j], 1)
+        else:
+            g.scalar.wait_ge(sem["ym%d" % j], 1)
+            g.scalar.activation(cols(T.yt, j), out, ActivationFunctionType.Copy).then_inc(sem["yc%d" % j], 1)
+    for i in range(4):
+        q = g.scalar if i == 3 else g.sync
+        f = first[i]
+        q.wait_ge(sem["yc%d" % f], 1)
+        q.wait_ge(sem["yc%d" % (f + 1)], 1)
+        q.dma_start(cols(T.y, f, C, 2), cols(T.yt, f, C, 2)).then_inc(sem.yst2 if i == 3 else sem.yst, 16)
+
+    g.scalar.wait_ge(sem.yst2, 16)
+    g.sync.wait_ge(sem.yst, 48)
+    g.sync.wait_ge(sem.hst, 16)
+    g.wait_ge(sem.sent1, sent1)
+    g.wait_ge(sem.sent2, sent2)

@@ -6,6 +6,15 @@ W = 512
 C = 128
 C2 = 0.328
 
+LOADS = [("sync", (2,)), ("scalar", (3,)), ("sync", (4, 5)), ("scalar", (6, 7)), ("sync", (0, 1))]
+UNITS = [(2,), (3,), (4, 5), (6, 7), (0, 1)]
+HOP = (2, 3)
+RS = [(t, ks) for ks in ((4, 5), (6,), (7,), (1,)) for t in "cs"]
+AG = [(t, ks) for ks in ((4, 5, 6, 7), (1,)) for t in "cs"]
+ZORDER = [0, 4, 5, 6, 7, 2, 1, 3]
+YORDER = [0, 4, 5, 6, 7, 1, 2, 3]
+STORES = [("sync", (4, 5)), ("sync", (6, 7)), ("sync", (0, 1)), ("scalar", (2, 3))]
+
 SCRATCH = {
     "bt": ("sbuf", [128, N * W], "bfloat16"),
     "xt": ("sbuf", [128, W], "bfloat16"),
@@ -19,90 +28,146 @@ SCRATCH = {
     "hq": ("sbuf", [128, N * C], "float8_e4m3fn_x4"), "hs": ("sbuf", [128, N * C], "uint8"),
     "ps": ("psum", [128, 8 * 512], "float32"),
 }
-SEMAPHORES = (["ld%d" % i for i in range(5)] + ["ldx", "ones", "eye", "sdone", "qx", "relu", "qh", "sent1", "sent2", "hst", "yst", "yst2"]
-              + ["qp%d" % i for i in range(4)] + ["z%d" % i for i in range(4)] + ["arr%d" % i for i in range(N)]
-              + ["har%d" % i for i in range(N)] + ["ym%d" % i for i in range(N)] + ["yc%d" % i for i in range(N)])
-
-PAIRS = [(2, 3), (4, 5), (6, 7), (1, 0)]
+SEMAPHORES = (["ldx", "go", "ones", "eye", "sdone", "qx", "relu", "qh", "sent1", "sent2", "hst"]
+              + [a + "%d" % i for a in ("ld", "qp", "arr", "har", "ym", "yc", "yst", "z") for i in range(N)])
 
 
 def rank_program(g, core, T, topo):
-    r = T.rank_of(core)
-    if r is None:
-        return
     sem = T.sem
+    queue = {"sync": g.sync, "scalar": g.scalar}
+    cores = list(T.cores)
+    sent = {"sent1": 0, "sent2": 0}
 
     def cols(t, i, w=C, n=1):
         return t[:, w * i:w * (i + n)]
 
-    def engines(dsts, parts):
+    def raw(kind, q, s, i):
+        return cols(T[q], i).bitcast(dt.uint8) if kind == "c" else cols(T[s], i)
+
+    def chip(c):
+        return topo.host(c), topo.chip(c)
+
+    def off_chip(src):
         m = 0xFFFFFFFF
-        for d in dsts:
-            m &= topo.mask(core, T.cores[d])
+        for d in cores:
+            if chip(d) != chip(src):
+                m &= topo.mask(src, d)
+        return m
+
+    def split(m, parts):
         bits = [i for i in range(m.bit_length()) if (m >> i) & 1]
         n = len(bits) // parts
         return [sum(1 << i for i in bits[p * n:(p + 1) * n]) for p in range(parts)], n
 
-    def dst_id(d):
-        rid, pid = topo.addr(T.cores[d], core)
+    def core_id(d):
+        rid, pid = topo.addr(d, core)
         return DstId(rid=rid, pnc=pid)
 
-    first = [min(r ^ a, r ^ b) for a, b in PAIRS]
+    def helper(c):
+        for d in range(256):
+            if chip(d) == chip(c) and topo.die(d) != topo.die(c) and all(topo.may_write(d, e) for e in cores):
+                return d
 
-    a = first[0]
-    g.sync.dma_start(cols(T.bt, a, W), cols(T.b, a, W)).then_inc(sem.ld0, 16)
-    g.scalar.dma_start(cols(T.bt, a + 1, W), cols(T.b, a + 1, W)).then_inc(sem.ld1, 16)
-    g.sync.dma_start(cols(T.bt, first[1], W, 2), cols(T.b, first[1], W, 2)).then_inc(sem.ld2, 16)
-    g.scalar.dma_start(cols(T.bt, first[2], W, 2), cols(T.b, first[2], W, 2)).then_inc(sem.ld3, 16)
-    g.sync.dma_start(cols(T.bt, first[3], W, 2), cols(T.b, first[3], W, 2)).then_inc(sem.ld4, 16)
+    def hop_engines(c):
+        (m,), n = split(topo.mask(c, helper(c)) & ~off_chip(c), 1)
+        return m, n
+
+    def scatter(r, kind, ks):
+        masks, n = split(off_chip(core), len(ks))
+        ts = []
+        for k, m in zip(ks, masks):
+            ts.append(RemoteDMATransfer(dst_ids=[core_id(cores[r ^ k])], srcs=[raw(kind, "gq", "gs", r ^ k)], dsts=[raw(kind, "lq", "ls", r)],
+                                        dma_engine_mask=m, remote_sem=sem["arr%d" % r], alu_op=0))
+            sent["sent1"] += n
+        g.remote_dma_fused(ts, local_sem=sem.sent1)
+
+    def gather(r, kind, ks):
+        (m,), n = split(off_chip(core), 1)
+        side = raw(kind, "hq", "hs", r)
+        g.remote_dma_fused([RemoteDMATransfer(dst_ids=[core_id(cores[r ^ k]) for k in ks], srcs=[side], dsts=[side for k in ks],
+                                              dma_engine_mask=m, remote_sem=sem["har%d" % r], alu_op=0)], local_sem=sem.sent2)
+        sent["sent2"] += n
+
+    def hop(kind, q, s, i, rsem, lsem):
+        m, n = hop_engines(core)
+        rid, pid = topo.addr(helper(core), core)
+        g.remote_dma(raw(kind, q, s, i), raw(kind, q, s, i), rsem, sem[lsem], pid, rid, m)
+        sent[lsem] += n
+
+    r = T.rank_of(core)
+    if r is None:
+        for i, c in enumerate(cores):
+            if helper(c) == core:
+                n = 2 * hop_engines(c)[1]
+                for k in HOP:
+                    g.wait_ge(sem["arr%d" % (i ^ k)], n)
+                    for kind in "cs":
+                        scatter(i, kind, (k,))
+                g.wait_ge(sem["har%d" % i], n)
+                for kind in "cs":
+                    gather(i, kind, HOP)
+                g.wait_ge(sem.sent1, sent["sent1"])
+                g.wait_ge(sem.sent2, sent["sent2"])
+        return
+
+    def run(ks):
+        return min(r ^ k for k in ks), len(ks)
+
+    loaded = {}
+    for i, (q, ks) in enumerate(LOADS):
+        f, n = run(ks)
+        queue[q].dma_start(cols(T.bt, f, W, n), cols(T.b, f, W, n)).then_inc(sem["ld%d" % i], 16)
+        for k in ks:
+            loaded[k] = i
+    g.scalar.wait_ge(sem.go, 1)
     g.scalar.dma_start(T.xt[:], T.x[:]).then_inc(sem.ldx, 16)
 
     g.vector.memset(T.eye[:], 1.0).then_inc(sem.ones, 1)
     g.wait_ge(sem.ones, 1)
     g.affine_select(T.eye[:], T.eye[:], [[-1, W + 4]], AluOpType.is_equal, 0.0, 3, 4).then_inc(sem.eye, 1)
 
-    for i in range(4):
-        if i == 0:
-            g.vector.wait_ge(sem.ld0, 16)
-            g.vector.wait_ge(sem.ld1, 16)
-        else:
-            g.vector.wait_ge(sem["ld%d" % (i + 1)], 16)
-        f = first[i]
-        g.vector.quantize_mx(cols(T.gq, f, C, 2), cols(T.gs, f, C, 2), cols(T.bt, f, W, 2)).then_inc(sem["qp%d" % i], 1)
-        if i == 1:
+    packed = {}
+    for i, ks in enumerate(UNITS):
+        for l in sorted(set(loaded[k] for k in ks)):
+            g.vector.wait_ge(sem["ld%d" % l], 16)
+        f, n = run(ks)
+        g.vector.quantize_mx(cols(T.gq, f, C, n), cols(T.gs, f, C, n), cols(T.bt, f, W, n)).then_inc(sem["qp%d" % i], 1)
+        for k in ks:
+            packed[k] = i
+        if i == 2:
             g.vector.wait_ge(sem.eye, 1)
             for b in range(4):
                 g.vector.quantize_mx(cols(T.sq, b), cols(T.ss, b), T.eye[:, 3 - b:3 - b + W]).then_inc(sem.sdone, 1)
-    g.vector.wait_ge(sem.ldx, 16)
-    g.vector.quantize_mx(T.xq[:], T.xs[:], T.xt[:]).then_inc(sem.qx, 1)
 
-    count = {}
-    sent1 = 0
-    for i in range(4):
-        dsts = [r ^ k for k in PAIRS[i] if k]
-        masks, n = engines(dsts, len(dsts))
-        g.wait_ge(sem["qp%d" % i], 1)
-        for codes in (True, False):
-            ts = []
-            for d, m in zip(dsts, masks):
-                src = cols(T.gq, d).bitcast(dt.uint8) if codes else cols(T.gs, d)
-                dst = cols(T.lq, r).bitcast(dt.uint8) if codes else cols(T.ls, r)
-                ts.append(RemoteDMATransfer(dst_ids=[dst_id(d)], srcs=[src], dsts=[dst], dma_engine_mask=m,
-                                            remote_sem=sem["arr%d" % r], alu_op=0))
-            g.remote_dma_fused(ts, local_sem=sem.sent1)
-            sent1 += n * len(dsts)
-        for k in PAIRS[i]:
-            count[k] = 2 * n
+    seen = []
+
+    def need(ks):
+        for k in ks:
+            if packed[k] not in seen:
+                seen.append(packed[k])
+                g.wait_ge(sem["qp%d" % packed[k]], 1)
+
+    full = split(off_chip(core), 1)[1]
+    count = {k: 2 * full for k in HOP}
+    for k in HOP:
+        need((k,))
+        for kind in "cs":
+            hop(kind, "gq", "gs", r ^ k, sem["arr%d" % (r ^ k)], "sent1")
+    for kind, ks in RS:
+        need(ks)
+        scatter(r, kind, ks)
+        for k in ks:
+            count[k] = 2 * full // len(ks)
+    g.sem_inc(sem.go, 1)
 
     g.tensor.wait_ge(sem.sdone, 4)
-    order = [2, 3, 0, 4, 5, 6, 7, 1]
-    for i, k in enumerate(order):
+    for i, k in enumerate(ZORDER):
         s = r ^ k
         if k:
             g.tensor.wait_ge(sem["arr%d" % s], count[k])
             q, p = cols(T.lq, s), cols(T.ls, s)
         else:
-            g.tensor.wait_ge(sem.qp3, 1)
+            g.tensor.wait_ge(sem["qp%d" % packed[0]], 1)
             q, p = cols(T.gq, s), cols(T.gs, s)
         for b in range(4):
             mm = g.tensor.matmul_mx(T.ps[:, 512 * b:512 * b + C], cols(T.sq, b), cols(T.ss, b), q, p, i == 0, i == N - 1)
@@ -112,7 +177,7 @@ def rank_program(g, core, T, topo):
     for b in range(4):
         z = T.ps[:, 512 * b:512 * b + C]
         o = T.ht[:, b:W:4]
-        if b % 2 == 0:
+        if b % 2:
             g.vector.wait_ge(sem["z%d" % b], 1)
             g.vector.tensor_scalar(o, z, 0.0, C2, AluOpType.max, AluOpType.mult).then_inc(sem.relu, 1)
         else:
@@ -120,47 +185,42 @@ def rank_program(g, core, T, topo):
             g.scalar.activation(o, z, ActivationFunctionType.Relu, scale=C2).then_inc(sem.relu, 1)
     g.vector.wait_ge(sem.relu, 4)
     g.vector.quantize_mx(cols(T.hq, r), cols(T.hs, r), T.ht[:]).then_inc(sem.qh, 1)
-    g.sync.wait_ge(sem.relu, 4)
-    g.sync.dma_start(T.h[:], T.ht[:]).then_inc(sem.hst, 16)
+    g.vector.wait_ge(sem.ldx, 16)
+    g.vector.quantize_mx(T.xq[:], T.xs[:], T.xt[:]).then_inc(sem.qx, 1)
 
     g.wait_ge(sem.qh, 1)
-    sent2 = 0
-    for ks in ((2, 3, 4, 5), (6, 7, 1)):
-        dsts = [r ^ k for k in ks]
-        masks, n = engines(dsts, 1)
-        for codes in (True, False):
-            side = cols(T.hq, r).bitcast(dt.uint8) if codes else cols(T.hs, r)
-            g.remote_dma_fused([RemoteDMATransfer(dst_ids=[dst_id(d) for d in dsts], srcs=[side], dsts=[side for d in dsts],
-                                                  dma_engine_mask=masks[0], remote_sem=sem["har%d" % r], alu_op=0)], local_sem=sem.sent2)
-            sent2 += n
-        got = 2 * n
+    for kind in "cs":
+        hop(kind, "hq", "hs", r, sem["har%d" % r], "sent2")
+    for kind, ks in AG:
+        gather(r, kind, ks)
 
-    order = [0, 2, 3, 4, 5, 6, 7, 1]
     g.tensor.wait_ge(sem.qx, 1)
-    for i, k in enumerate(order):
+    for i, k in enumerate(YORDER):
         j = r ^ k
         bank = (i + 4) % 8
         out = T.ps[:, 512 * bank:512 * bank + C]
         if k:
-            g.tensor.wait_ge(sem["har%d" % j], got)
+            g.tensor.wait_ge(sem["har%d" % j], 2 * full)
         else:
             g.tensor.wait_ge(sem.qh, 1)
         g.tensor.matmul_mx(out, cols(T.hq, j), cols(T.hs, j), T.xq[:], T.xs[:], True, True).then_inc(sem["ym%d" % j], 1)
-        if i % 2 == 0:
+        if i % 2:
             g.vector.wait_ge(sem["ym%d" % j], 1)
             g.vector.tensor_copy(cols(T.yt, j), out).then_inc(sem["yc%d" % j], 1)
         else:
             g.scalar.wait_ge(sem["ym%d" % j], 1)
             g.scalar.activation(cols(T.yt, j), out, ActivationFunctionType.Copy).then_inc(sem["yc%d" % j], 1)
-    for i in range(4):
-        q = g.scalar if i == 3 else g.sync
-        f = first[i]
-        q.wait_ge(sem["yc%d" % f], 1)
-        q.wait_ge(sem["yc%d" % (f + 1)], 1)
-        q.dma_start(cols(T.y, f, C, 2), cols(T.yt, f, C, 2)).then_inc(sem.yst2 if i == 3 else sem.yst, 16)
+    for i, (q, ks) in enumerate(STORES):
+        f, n = run(ks)
+        for k in ks:
+            queue[q].wait_ge(sem["yc%d" % (r ^ k)], 1)
+        queue[q].dma_start(cols(T.y, f, C, n), cols(T.yt, f, C, n)).then_inc(sem["yst%d" % i], 16)
+        if i == 0:
+            g.sync.wait_ge(sem.relu, 4)
+            g.sync.dma_start(T.h[:], T.ht[:]).then_inc(sem.hst, 16)
 
-    g.scalar.wait_ge(sem.yst2, 16)
-    g.sync.wait_ge(sem.yst, 48)
+    for i, (q, ks) in enumerate(STORES):
+        queue[q].wait_ge(sem["yst%d" % i], 16)
     g.sync.wait_ge(sem.hst, 16)
-    g.wait_ge(sem.sent1, sent1)
-    g.wait_ge(sem.sent2, sent2)
+    g.wait_ge(sem.sent1, sent["sent1"])
+    g.wait_ge(sem.sent2, sent["sent2"])

@@ -6,18 +6,22 @@ W = 512
 C = 128
 C2 = 0.328
 
-LOADS = [("sync", (2,)), ("scalar", (3,)), ("sync", (4, 5)), ("scalar", (6, 7)), ("sync", (0, 1))]
-UNITS = [(2,), (3,), (4, 5), (6, 7), (0, 1)]
-HOP = (2, 3)
-RS = [(t, ks) for ks in ((4, 5), (6,), (7,), (1,)) for t in "cs"]
-AG = [(t, ks) for ks in ((4, 5, 6, 7), (1,)) for t in "cs"]
-ZORDER = [0, 4, 5, 6, 7, 2, 1, 3]
-YORDER = [0, 4, 5, 6, 7, 1, 2, 3]
+LOADS = [("sync", (2, 3)), ("scalar", (1,)), ("sync", (4, 5)), ("scalar", (0,)), ("sync", (6, 7))]
+UNITS = [2, 3, 1, 5, 4, 0, 6, 7]
+HELPERS = [(False, (0,), (2,), ()), (False, (1,), (4, 6), (7, 3)), (True, (2,), (), (1,))]
+RS = [(2, 0), (3, None), (1, None), (5, None), (4, 1), (6, 1), (7, None)]
+X_AFTER = 5
+HOP = (1, 2)
+AG = (4, 5, 6, 2)
+ZORDER = [0, 3, 1, 5, 2, 4, 7, 6]
+YORDER = [0, 4, 5, 7, 6, 1, 3, 2]
 STORES = [("sync", (4, 5)), ("sync", (6, 7)), ("sync", (0, 1)), ("scalar", (2, 3))]
+KINDS = "sc"
 
 SCRATCH = {
     "bt": ("sbuf", [128, N * W], "bfloat16"),
     "xt": ("sbuf", [128, W], "bfloat16"),
+    "one": ("sbuf", [128, C], "bfloat16"),
     "eye": ("sbuf", [128, W + 4], "bfloat16"),
     "ht": ("sbuf", [128, W], "bfloat16"),
     "yt": ("sbuf", [128, N * C], "float32"),
@@ -28,86 +32,99 @@ SCRATCH = {
     "hq": ("sbuf", [128, N * C], "float8_e4m3fn_x4"), "hs": ("sbuf", [128, N * C], "uint8"),
     "ps": ("psum", [128, 8 * 512], "float32"),
 }
-SEMAPHORES = (["ldx", "go", "ones", "eye", "sdone", "qx", "relu", "qh", "sent1", "sent2", "hst"]
-              + [a + "%d" % i for a in ("ld", "qp", "arr", "har", "ym", "yc", "yst", "z") for i in range(N)])
+SEMAPHORES = (["ldx", "go", "fill", "eye", "sdone", "sel", "qx", "relu", "qh", "sent0", "sent1", "sent2", "hst", "hopc", "hops"]
+              + [a + "%d" % i for a in ("ld", "qp", "arr", "har", "ym", "yc", "yst", "z", "tc", "ts") for i in range(N)])
 
 
 def rank_program(g, core, T, topo):
     sem = T.sem
     queue = {"sync": g.sync, "scalar": g.scalar}
     cores = list(T.cores)
-    sent = {"sent1": 0, "sent2": 0}
+    sent = {"sent0": 0, "sent1": 0, "sent2": 0}
 
     def cols(t, i, w=C, n=1):
         return t[:, w * i:w * (i + n)]
 
-    def raw(kind, q, s, i):
-        return cols(T[q], i).bitcast(dt.uint8) if kind == "c" else cols(T[s], i)
+    def raw(kind, q, s, i, n=1):
+        return cols(T[q], i, C, n).bitcast(dt.uint8) if kind == "c" else cols(T[s], i, C, n)
 
     def chip(c):
         return topo.host(c), topo.chip(c)
 
+    def size(m):
+        return bin(m).count("1")
+
     def off_chip(src):
         m = 0xFFFFFFFF
         for d in cores:
-            if chip(d) != chip(src):
+            if chip(d) != chip(src) and topo.may_write(src, d):
                 m &= topo.mask(src, d)
         return m
 
-    def split(m, parts):
-        bits = [i for i in range(m.bit_length()) if (m >> i) & 1]
-        n = len(bits) // parts
-        return [sum(1 << i for i in bits[p * n:(p + 1) * n]) for p in range(parts)], n
-
-    def core_id(d):
+    def address(d):
         rid, pid = topo.addr(d, core)
         return DstId(rid=rid, pnc=pid)
 
-    def helper(c):
-        for d in range(256):
-            if chip(d) == chip(c) and topo.die(d) != topo.die(c) and all(topo.may_write(d, e) for e in cores):
-                return d
+    def send(side_out, side_in, dests, rsem, lsem, m):
+        g.remote_dma_fused([RemoteDMATransfer(dst_ids=[address(d) for d in dests], srcs=[side_in], dsts=[side_out for d in dests],
+                                              dma_engine_mask=m, remote_sem=rsem, alu_op=0)], local_sem=sem[lsem])
+        sent[lsem] += size(m)
 
-    def hop_engines(c):
-        (m,), n = split(topo.mask(c, helper(c)) & ~off_chip(c), 1)
-        return m, n
+    def helpers(i):
+        out = []
+        for own, _, rs, ag in HELPERS:
+            out.append([d for d in range(256) if chip(d) == chip(cores[i]) and d != cores[i] and d not in out
+                        and (topo.die(d) == topo.die(cores[i])) == own
+                        and all(topo.may_write(d, cores[i ^ k]) for k in rs + ag)][0])
+        return out
 
-    def scatter(r, kind, ks):
-        masks, n = split(off_chip(core), len(ks))
-        ts = []
-        for k, m in zip(ks, masks):
-            ts.append(RemoteDMATransfer(dst_ids=[core_id(cores[r ^ k])], srcs=[raw(kind, "gq", "gs", r ^ k)], dsts=[raw(kind, "lq", "ls", r)],
-                                        dma_engine_mask=m, remote_sem=sem["arr%d" % r], alu_op=0))
-            sent["sent1"] += n
-        g.remote_dma_fused(ts, local_sem=sem.sent1)
+    def hop_engines(i, h):
+        return topo.mask(cores[i], h) & ~off_chip(cores[i])
 
-    def gather(r, kind, ks):
-        (m,), n = split(off_chip(core), 1)
-        side = raw(kind, "hq", "hs", r)
-        g.remote_dma_fused([RemoteDMATransfer(dst_ids=[core_id(cores[r ^ k]) for k in ks], srcs=[side], dsts=[side for k in ks],
-                                              dma_engine_mask=m, remote_sem=sem["har%d" % r], alu_op=0)], local_sem=sem.sent2)
-        sent["sent2"] += n
+    def scatter(i, kind, k):
+        send(raw(kind, "lq", "ls", i), raw(kind, "gq", "gs", i ^ k), [cores[i ^ k]], sem["arr%d" % i], "sent1", off_chip(core))
 
-    def hop(kind, q, s, i, rsem, lsem):
-        m, n = hop_engines(core)
-        rid, pid = topo.addr(helper(core), core)
-        g.remote_dma(raw(kind, q, s, i), raw(kind, q, s, i), rsem, sem[lsem], pid, rid, m)
-        sent[lsem] += n
+    def gather(i, kind, ks):
+        side = raw(kind, "hq", "hs", i)
+        send(side, side, [cores[i ^ k] for k in ks], sem["har%d" % i], "sent2", off_chip(core))
 
+    def select(bs):
+        g.vector.memset(T.one[:], 1.0).then_inc(sem.fill, 1)
+        g.vector.memset(T.eye[:], 0.0).then_inc(sem.fill, 1)
+        g.wait_ge(sem.fill, 2)
+        g.affine_select(T.eye[:, 3:3 + W:4], T.one[:], [[-1, C]], AluOpType.is_equal, 0.0, 0, 1).then_inc(sem.eye, 1)
+        g.vector.wait_ge(sem.eye, 1)
+        for b in bs:
+            g.vector.quantize_mx(cols(T.sq, b), cols(T.ss, b), T.eye[:, 3 - b:3 - b + W]).then_inc(sem.sdone, 1)
+
+    mine = [i for i, c in enumerate(cores) if chip(c) == chip(core)]
+    if not mine:
+        return
+    home = mine[0]
+    team = helpers(home)
     r = T.rank_of(core)
+
     if r is None:
-        for i, c in enumerate(cores):
-            if helper(c) == core:
-                n = 2 * hop_engines(c)[1]
-                for k in HOP:
-                    g.wait_ge(sem["arr%d" % (i ^ k)], n)
-                    for kind in "cs":
-                        scatter(i, kind, (k,))
-                g.wait_ge(sem["har%d" % i], n)
-                for kind in "cs":
-                    gather(i, kind, HOP)
-                g.wait_ge(sem.sent1, sent["sent1"])
-                g.wait_ge(sem.sent2, sent["sent2"])
+        if core not in team:
+            return
+        own, sels, rs, ag = HELPERS[team.index(core)]
+        hop = size(hop_engines(home, core))
+        select(sels)
+        g.wait_ge(sem.sdone, len(sels))
+        for kind in KINDS:
+            side = raw(kind, "sq", "ss", sels[0], len(sels))
+            send(side, side, [cores[home]], sem.sel, "sent0", topo.mask(core, cores[home]))
+        for k in rs:
+            for kind in KINDS:
+                g.wait_ge(sem["t%s%d" % (kind, home ^ k)], hop)
+                scatter(home, kind, k)
+        if ag:
+            for kind in KINDS:
+                g.wait_ge(sem["hop" + kind], hop)
+                gather(home, kind, ag)
+        for s in ("sent0", "sent1", "sent2"):
+            if sent[s]:
+                g.wait_ge(sem[s], sent[s])
         return
 
     def run(ks):
@@ -122,52 +139,34 @@ def rank_program(g, core, T, topo):
     g.scalar.wait_ge(sem.go, 1)
     g.scalar.dma_start(T.xt[:], T.x[:]).then_inc(sem.ldx, 16)
 
-    g.vector.memset(T.eye[:], 1.0).then_inc(sem.ones, 1)
-    g.wait_ge(sem.ones, 1)
-    g.affine_select(T.eye[:], T.eye[:], [[-1, W + 4]], AluOpType.is_equal, 0.0, 3, 4).then_inc(sem.eye, 1)
+    left = [b for b in range(4) if all(b not in h[1] for h in HELPERS)]
+    select(left)
 
-    packed = {}
-    for i, ks in enumerate(UNITS):
-        for l in sorted(set(loaded[k] for k in ks)):
-            g.vector.wait_ge(sem["ld%d" % l], 16)
-        f, n = run(ks)
-        g.vector.quantize_mx(cols(T.gq, f, C, n), cols(T.gs, f, C, n), cols(T.bt, f, W, n)).then_inc(sem["qp%d" % i], 1)
-        for k in ks:
-            packed[k] = i
-        if i == 2:
-            g.vector.wait_ge(sem.eye, 1)
-            for b in range(4):
-                g.vector.quantize_mx(cols(T.sq, b), cols(T.ss, b), T.eye[:, 3 - b:3 - b + W]).then_inc(sem.sdone, 1)
+    for k in UNITS:
+        t = r ^ k
+        g.vector.wait_ge(sem["ld%d" % loaded[k]], 16)
+        g.vector.quantize_mx(cols(T.gq, t), cols(T.gs, t), cols(T.bt, t, W)).then_inc(sem["qp%d" % k], 1)
+    for i, (k, j) in enumerate(RS):
+        if i == X_AFTER:
+            g.sem_inc(sem.go, 1)
+        g.wait_ge(sem["qp%d" % k], 1)
+        for kind in KINDS:
+            if j is None:
+                scatter(r, kind, k)
+            else:
+                side = raw(kind, "gq", "gs", r ^ k)
+                send(side, side, [team[j]], sem["t%s%d" % (kind, r ^ k)], "sent1", hop_engines(r, team[j]))
 
-    seen = []
-
-    def need(ks):
-        for k in ks:
-            if packed[k] not in seen:
-                seen.append(packed[k])
-                g.wait_ge(sem["qp%d" % packed[k]], 1)
-
-    full = split(off_chip(core), 1)[1]
-    count = {k: 2 * full for k in HOP}
-    for k in HOP:
-        need((k,))
-        for kind in "cs":
-            hop(kind, "gq", "gs", r ^ k, sem["arr%d" % (r ^ k)], "sent1")
-    for kind, ks in RS:
-        need(ks)
-        scatter(r, kind, ks)
-        for k in ks:
-            count[k] = 2 * full // len(ks)
-    g.sem_inc(sem.go, 1)
-
-    g.tensor.wait_ge(sem.sdone, 4)
+    full = 2 * size(off_chip(core))
+    g.tensor.wait_ge(sem.sdone, len(left))
+    g.tensor.wait_ge(sem.sel, sum(2 * size(topo.mask(h, core)) for h in team))
     for i, k in enumerate(ZORDER):
         s = r ^ k
         if k:
-            g.tensor.wait_ge(sem["arr%d" % s], count[k])
+            g.tensor.wait_ge(sem["arr%d" % s], full)
             q, p = cols(T.lq, s), cols(T.ls, s)
         else:
-            g.tensor.wait_ge(sem["qp%d" % packed[0]], 1)
+            g.tensor.wait_ge(sem["qp%d" % k], 1)
             q, p = cols(T.gq, s), cols(T.gs, s)
         for b in range(4):
             mm = g.tensor.matmul_mx(T.ps[:, 512 * b:512 * b + C], cols(T.sq, b), cols(T.ss, b), q, p, i == 0, i == N - 1)
@@ -189,10 +188,12 @@ def rank_program(g, core, T, topo):
     g.vector.quantize_mx(T.xq[:], T.xs[:], T.xt[:]).then_inc(sem.qx, 1)
 
     g.wait_ge(sem.qh, 1)
-    for kind in "cs":
-        hop(kind, "hq", "hs", r, sem["har%d" % r], "sent2")
-    for kind, ks in AG:
-        gather(r, kind, ks)
+    for kind in KINDS:
+        side = raw(kind, "hq", "hs", r)
+        send(side, side, [team[j] for j in HOP], sem["hop" + kind], "sent2", hop_engines(r, team[HOP[0]]))
+    for k in AG:
+        for kind in KINDS:
+            gather(r, kind, (k,))
 
     g.tensor.wait_ge(sem.qx, 1)
     for i, k in enumerate(YORDER):
@@ -200,7 +201,7 @@ def rank_program(g, core, T, topo):
         bank = (i + 4) % 8
         out = T.ps[:, 512 * bank:512 * bank + C]
         if k:
-            g.tensor.wait_ge(sem["har%d" % j], 2 * full)
+            g.tensor.wait_ge(sem["har%d" % j], full)
         else:
             g.tensor.wait_ge(sem.qh, 1)
         g.tensor.matmul_mx(out, cols(T.hq, j), cols(T.hs, j), T.xq[:], T.xs[:], True, True).then_inc(sem["ym%d" % j], 1)

from concourse.bass import DstId, RemoteDMATransfer
from concourse.mybir import dt, AluOpType, ActivationFunctionType

N = 8
W = 512
C = 128
C2 = 0.328

LOADS = [("sync", (2, 3)), ("scalar", (1,)), ("sync", (4, 5)), ("scalar", (0,)), ("sync", (6, 7))]
UNITS = [2, 3, 1, 5, 4, 0, 6, 7]
HELPERS = [(False, (0,), (2,), ()), (False, (1,), (4, 6), (7, 3)), (True, (2,), (), (1,))]
RS = [(2, 0), (3, None), (1, None), (5, None), (4, 1), (6, 1), (7, None)]
X_AFTER = 5
HOP = (1, 2)
AG = (4, 5, 6, 2)
ZORDER = [0, 3, 1, 5, 2, 4, 7, 6]
YORDER = [0, 4, 5, 7, 6, 1, 3, 2]
STORES = [("sync", (4, 5)), ("sync", (6, 7)), ("sync", (0, 1)), ("scalar", (2, 3))]
KINDS = "sc"

SCRATCH = {
    "bt": ("sbuf", [128, N * W], "bfloat16"),
    "xt": ("sbuf", [128, W], "bfloat16"),
    "one": ("sbuf", [128, C], "bfloat16"),
    "eye": ("sbuf", [128, W + 4], "bfloat16"),
    "ht": ("sbuf", [128, W], "bfloat16"),
    "yt": ("sbuf", [128, N * C], "float32"),
    "xq": ("sbuf", [128, C], "float8_e4m3fn_x4"), "xs": ("sbuf", [128, C], "uint8"),
    "sq": ("sbuf", [128, 4 * C], "float8_e4m3fn_x4"), "ss": ("sbuf", [128, 4 * C], "uint8"),
    "gq": ("sbuf", [128, N * C], "float8_e4m3fn_x4"), "gs": ("sbuf", [128, N * C], "uint8"),
    "lq": ("sbuf", [128, N * C], "float8_e4m3fn_x4"), "ls": ("sbuf", [128, N * C], "uint8"),
    "hq": ("sbuf", [128, N * C], "float8_e4m3fn_x4"), "hs": ("sbuf", [128, N * C], "uint8"),
    "ps": ("psum", [128, 8 * 512], "float32"),
}
SEMAPHORES = (["ldx", "go", "fill", "eye", "sdone", "sel", "qx", "relu", "qh", "sent0", "sent1", "sent2", "hst", "hopc", "hops"]
              + [a + "%d" % i for a in ("ld", "qp", "arr", "har", "ym", "yc", "yst", "z", "tc", "ts") for i in range(N)])


def rank_program(g, core, T, topo):
    sem = T.sem
    queue = {"sync": g.sync, "scalar": g.scalar}
    cores = list(T.cores)
    sent = {"sent0": 0, "sent1": 0, "sent2": 0}

    def cols(t, i, w=C, n=1):
        return t[:, w * i:w * (i + n)]

    def raw(kind, q, s, i, n=1):
        return cols(T[q], i, C, n).bitcast(dt.uint8) if kind == "c" else cols(T[s], i, C, n)

    def chip(c):
        return topo.host(c), topo.chip(c)

    def size(m):
        return bin(m).count("1")

    def off_chip(src):
        m = 0xFFFFFFFF
        for d in cores:
            if chip(d) != chip(src) and topo.may_write(src, d):
                m &= topo.mask(src, d)
        return m

    def address(d):
        rid, pid = topo.addr(d, core)
        return DstId(rid=rid, pnc=pid)

    def send(side_out, side_in, dests, rsem, lsem, m):
        g.remote_dma_fused([RemoteDMATransfer(dst_ids=[address(d) for d in dests], srcs=[side_in], dsts=[side_out for d in dests],
                                              dma_engine_mask=m, remote_sem=rsem, alu_op=0)], local_sem=sem[lsem])
        sent[lsem] += size(m)

    def helpers(i):
        out = []
        for own, _, rs, ag in HELPERS:
            out.append([d for d in range(256) if chip(d) == chip(cores[i]) and d != cores[i] and d not in out
                        and (topo.die(d) == topo.die(cores[i])) == own
                        and all(topo.may_write(d, cores[i ^ k]) for k in rs + ag)][0])
        return out

    def hop_engines(i, h):
        return topo.mask(cores[i], h) & ~off_chip(cores[i])

    def scatter(i, kind, k):
        send(raw(kind, "lq", "ls", i), raw(kind, "gq", "gs", i ^ k), [cores[i ^ k]], sem["arr%d" % i], "sent1", off_chip(core))

    def gather(i, kind, ks):
        side = raw(kind, "hq", "hs", i)
        send(side, side, [cores[i ^ k] for k in ks], sem["har%d" % i], "sent2", off_chip(core))

    def select(bs):
        g.vector.memset(T.one[:], 1.0).then_inc(sem.fill, 1)
        g.vector.memset(T.eye[:], 0.0).then_inc(sem.fill, 1)
        g.wait_ge(sem.fill, 2)
        g.affine_select(T.eye[:, 3:3 + W:4], T.one[:], [[-1, C]], AluOpType.is_equal, 0.0, 0, 1).then_inc(sem.eye, 1)
        g.vector.wait_ge(sem.eye, 1)
        for b in bs:
            g.vector.quantize_mx(cols(T.sq, b), cols(T.ss, b), T.eye[:, 3 - b:3 - b + W]).then_inc(sem.sdone, 1)

    mine = [i for i, c in enumerate(cores) if chip(c) == chip(core)]
    if not mine:
        return
    home = mine[0]
    team = helpers(home)
    r = T.rank_of(core)

    if r is None:
        if core not in team:
            return
        own, sels, rs, ag = HELPERS[team.index(core)]
        hop = size(hop_engines(home, core))
        select(sels)
        g.wait_ge(sem.sdone, len(sels))
        for kind in KINDS:
            side = raw(kind, "sq", "ss", sels[0], len(sels))
            send(side, side, [cores[home]], sem.sel, "sent0", topo.mask(core, cores[home]))
        for k in rs:
            for kind in KINDS:
                g.wait_ge(sem["t%s%d" % (kind, home ^ k)], hop)
                scatter(home, kind, k)
        if ag:
            for kind in KINDS:
                g.wait_ge(sem["hop" + kind], hop)
                gather(home, kind, ag)
        for s in ("sent0", "sent1", "sent2"):
            if sent[s]:
                g.wait_ge(sem[s], sent[s])
        return

    def run(ks):
        return min(r ^ k for k in ks), len(ks)

    loaded = {}
    for i, (q, ks) in enumerate(LOADS):
        f, n = run(ks)
        queue[q].dma_start(cols(T.bt, f, W, n), cols(T.b, f, W, n)).then_inc(sem["ld%d" % i], 16)
        for k in ks:
            loaded[k] = i
    g.scalar.wait_ge(sem.go, 1)
    g.scalar.dma_start(T.xt[:], T.x[:]).then_inc(sem.ldx, 16)

    left = [b for b in range(4) if all(b not in h[1] for h in HELPERS)]
    select(left)

    for k in UNITS:
        t = r ^ k
        g.vector.wait_ge(sem["ld%d" % loaded[k]], 16)
        g.vector.quantize_mx(cols(T.gq, t), cols(T.gs, t), cols(T.bt, t, W)).then_inc(sem["qp%d" % k], 1)
    for i, (k, j) in enumerate(RS):
        if i == X_AFTER:
            g.sem_inc(sem.go, 1)
        g.wait_ge(sem["qp%d" % k], 1)
        for kind in KINDS:
            if j is None:
                scatter(r, kind, k)
            else:
                side = raw(kind, "gq", "gs", r ^ k)
                send(side, side, [team[j]], sem["t%s%d" % (kind, r ^ k)], "sent1", hop_engines(r, team[j]))

    full = 2 * size(off_chip(core))
    g.tensor.wait_ge(sem.sdone, len(left))
    g.tensor.wait_ge(sem.sel, sum(2 * size(topo.mask(h, core)) for h in team))
    for i, k in enumerate(ZORDER):
        s = r ^ k
        if k:
            g.tensor.wait_ge(sem["arr%d" % s], full)
            q, p = cols(T.lq, s), cols(T.ls, s)
        else:
            g.tensor.wait_ge(sem["qp%d" % k], 1)
            q, p = cols(T.gq, s), cols(T.gs, s)
        for b in range(4):
            mm = g.tensor.matmul_mx(T.ps[:, 512 * b:512 * b + C], cols(T.sq, b), cols(T.ss, b), q, p, i == 0, i == N - 1)
            if i == N - 1:
                mm.then_inc(sem["z%d" % b], 1)

    for b in range(4):
        z = T.ps[:, 512 * b:512 * b + C]
        o = T.ht[:, b:W:4]
        if b % 2:
            g.vector.wait_ge(sem["z%d" % b], 1)
            g.vector.tensor_scalar(o, z, 0.0, C2, AluOpType.max, AluOpType.mult).then_inc(sem.relu, 1)
        else:
            g.scalar.wait_ge(sem["z%d" % b], 1)
            g.scalar.activation(o, z, ActivationFunctionType.Relu, scale=C2).then_inc(sem.relu, 1)
    g.vector.wait_ge(sem.relu, 4)
    g.vector.quantize_mx(cols(T.hq, r), cols(T.hs, r), T.ht[:]).then_inc(sem.qh, 1)
    g.vector.wait_ge(sem.ldx, 16)
    g.vector.quantize_mx(T.xq[:], T.xs[:], T.xt[:]).then_inc(sem.qx, 1)

    g.wait_ge(sem.qh, 1)
    for kind in KINDS:
        side = raw(kind, "hq", "hs", r)
        send(side, side, [team[j] for j in HOP], sem["hop" + kind], "sent2", hop_engines(r, team[HOP[0]]))
    for k in AG:
        for kind in KINDS:
            gather(r, kind, (k,))

    g.tensor.wait_ge(sem.qx, 1)
    for i, k in enumerate(YORDER):
        j = r ^ k
        bank = (i + 4) % 8
        out = T.ps[:, 512 * bank:512 * bank + C]
        if k:
            g.tensor.wait_ge(sem["har%d" % j], full)
        else:
            g.tensor.wait_ge(sem.qh, 1)
        g.tensor.matmul_mx(out, cols(T.hq, j), cols(T.hs, j), T.xq[:], T.xs[:], True, True).then_inc(sem["ym%d" % j], 1)
        if i % 2:
            g.vector.wait_ge(sem["ym%d" % j], 1)
            g.vector.tensor_copy(cols(T.yt, j), out).then_inc(sem["yc%d" % j], 1)
        else:
            g.scalar.wait_ge(sem["ym%d" % j], 1)
            g.scalar.activation(cols(T.yt, j), out, ActivationFunctionType.Copy).then_inc(sem["yc%d" % j], 1)
    for i, (q, ks) in enumerate(STORES):
        f, n = run(ks)
        for k in ks:
            queue[q].wait_ge(sem["yc%d" % (r ^ k)], 1)
        queue[q].dma_start(cols(T.y, f, C, n), cols(T.yt, f, C, n)).then_inc(sem["yst%d" % i], 16)
        if i == 0:
            g.sync.wait_ge(sem.relu, 4)
            g.sync.dma_start(T.h[:], T.ht[:]).then_inc(sem.hst, 16)

    for i, (q, ks) in enumerate(STORES):
        queue[q].wait_ge(sem["yst%d" % i], 16)
    g.sync.wait_ge(sem.hst, 16)
    g.wait_ge(sem.sent1, sent["sent1"])
    g.wait_ge(sem.sent2, sent["sent2"])
